import numpy as np, ml_dtypes
CORES = [8,11,14,16,19,22,24,27,30]
N = 9
WB, KB, QP = 1, 4, 64
def setup_inputs(rng):
    return {"q": rng.standard_normal((N, 128, QP), dtype=np.float32).astype(ml_dtypes.bfloat16), "k": rng.standard_normal((N, 128, KB * 128), dtype=np.float32).astype(ml_dtypes.bfloat16), "v": rng.standard_normal((N, 128, KB * 128), dtype=np.float32).astype(ml_dtypes.bfloat16)}
def setup_inputs_big(rng):
    d = setup_inputs(rng)
    for k in ("q", "k", "v"): d[k] = (d[k].astype(np.float32) * 1024.0).astype(d[k].dtype)
    return d
def setup_inputs_small(rng):
    d = setup_inputs(rng)
    for k in ("q", "k", "v"): d[k] = (d[k].astype(np.float32) * (1 / 1024.0)).astype(d[k].dtype)
    return d
def setup_inputs_apart(rng):
    d = setup_inputs(rng)
    f = (10.0 ** rng.permutation(np.linspace(-1.5, 1.5, N))).astype(np.float32).reshape(N, 1, 1)
    for k in ("q", "k", "v"): d[k] = (d[k].astype(np.float32) * f).astype(d[k].dtype)
    return d
def reference(q, k, v):
    Q, K, V = q.astype(np.float64), k.astype(np.float64), v.astype(np.float64)
    y = np.zeros((N, 128, QP))
    for r in range(N):
        for j in range(max(0, r - WB), r + 1):
            for b in range(KB):
                S = np.maximum(K[j][:, 128 * b:128 * b + 128].T @ Q[r], 0.0)
                y[r] += V[j][:, 128 * b:128 * b + 128].T @ S
    return {"y": y.astype(ml_dtypes.bfloat16 if q.dtype != np.float64 else np.float64)}

@@ -1,0 +1,148 @@
+from concourse.mybir import AluOpType
+
+QP, KB = 64, 4
+N_STAGE = 4
+N_ROWS = 8
+
+SCRATCH = {
+    "qd": ("dram", [128, QP], "bfloat16"),
+    "qr": ("dram", [128, QP], "bfloat16"),
+    "qs": ("sbuf", [128, QP], "bfloat16"),
+    "ks": ("sbuf", [128, KB * 128], "bfloat16"),
+    "vs": ("sbuf", [128, KB * 128], "bfloat16"),
+    "qn": ("sbuf", [128, QP], "bfloat16"),
+    "zero": ("sbuf", [128, KB * QP], "float32"),
+    "so_sb": ("sbuf", [128, KB * QP], "bfloat16"),
+    "sn_sb": ("sbuf", [128, KB * QP], "bfloat16"),
+    "on_sb": ("sbuf", [128, QP], "bfloat16"),
+    "land": ("sbuf", [128, QP], "bfloat16"),
+    "ys": ("sbuf", [128, QP], "bfloat16"),
+    "p_so": ("psum", [128, 512], "float32"),
+    "p_oo": ("psum", [128, 512], "float32"),
+    "p_on": ("psum", [128, 512], "float32"),
+    "p_sn0": ("psum", [128, 512], "float32"),
+    "p_sn1": ("psum", [128, 512], "float32"),
+    "p_sn2": ("psum", [128, 512], "float32"),
+    "p_sn3": ("psum", [128, 512], "float32"),
+}
+SEMAPHORES = ["qd", "q", "k", "v", "z", "so", "ro", "oo", "qn", "on", "cp", "land", "y", "st", "loc", "rel",
+              "sn0", "sn1", "sn2", "sn3", "rn0", "rn1", "rn2", "rn3"]
+
+
+def _routes(T, topo):
+    routes = {}
+    for r in range(1, len(T.cores)):
+        src, dst = T.cores[r], T.cores[r - 1]
+        if topo.may_write(src, dst):
+            routes[r] = [src, dst]
+        else:
+            cands = [c for c in T.cores[1:] if c != src and c != dst
+                     and topo.chip(c) == topo.chip(src) and topo.may_write(c, dst)]
+            cands.sort(key=lambda c: (topo.die(c) != topo.die(src), c))
+            routes[r] = [src, cands[0], dst]
+    return routes
+
+
+def _engines(T, topo, routes, core, n):
+    dests = []
+    for way in routes.values():
+        for a, b in zip(way[:-1], way[1:]):
+            if a == core:
+                dests.append(b)
+    r = T.rank_of(core)
+    if r + 1 < len(T.cores):
+        dests.append(T.cores[r + 1])
+    common = -1
+    for d in dests:
+        common &= topo.mask(core, d)
+    out, got, bit = 0, 0, 1
+    while got < n:
+        if common & bit:
+            out |= bit
+            got += 1
+        bit <<= 1
+    return out
+
+
+def rank_program(g, core, T, topo):
+    rank = T.rank_of(core)
+    if rank is None:
+        return
+    S = T.sem
+    n = len(T.cores)
+    has_prev, has_next = rank > 0, rank + 1 < n
+    routes = _routes(T, topo)
+    passes = [way for way in routes.values() if len(way) == 3 and way[1] == core]
+
+    def send(dst_core, out_ap, in_ap, sem, n_eng):
+        rid, pid, _ = topo.addr(dst_core)
+        g.remote_dma(out_ap, in_ap, sem, S.loc, pid, rid, _engines(T, topo, routes, core, n_eng))
+        return n_eng
+
+    if has_prev:
+        g.sync.dma_start(T.qd[0:64, :], T.q[0:64, :]).then_inc(S.qd, 16)
+        g.scalar.dma_start(T.qd[64:128, :], T.q[64:128, :]).then_inc(S.qd, 16)
+    g.sync.dma_start(T.qs[:], T.q[:]).then_inc(S.q, 16)
+    g.sync.dma_start(T.ks[:], T.k[:]).then_inc(S.k, 16)
+    g.scalar.dma_start(T.vs[:], T.v[:]).then_inc(S.v, 16)
+
+    left = 0
+    if has_prev:
+        way = routes[rank]
+        g.wait_ge(S.qd, 32)
+        if len(way) == 2:
+            left += send(way[1], T.qn[:], T.qd[:], S.qn, N_ROWS)
+        else:
+            left += send(way[1], T.qr[:], T.qd[:], S.rel, N_STAGE)
+    for way in passes:
+        g.wait_ge(S.rel, N_STAGE)
+        left += send(way[2], T.qn[:], T.qr[:], S.qn, N_ROWS)
+    if has_next:
+        g.wait_ge(S.cp, 1)
+        left += send(T.cores[rank + 1], T.land[:], T.on_sb[:], S.land, N_ROWS)
+    if left:
+        g.wait_ge(S.loc, left)
+
+    te = g.tensor
+    te.wait_ge(S.q, 16)
+    te.wait_ge(S.k, 16)
+    for b in range(KB):
+        te.matmul(T.p_so[:, QP * b:QP * (b + 1)], T.ks[:, 128 * b:128 * (b + 1)], T.qs[:],
+                  start=True, stop=True).then_inc(S.so, 1)
+    te.wait_ge(S.v, 16)
+    te.wait_ge(S.ro, 1)
+    for b in range(KB):
+        te.matmul(T.p_oo[:, 0:QP], T.vs[:, 128 * b:128 * (b + 1)], T.so_sb[:, QP * b:QP * (b + 1)],
+                  start=(b == 0), stop=(b == KB - 1)).then_inc(S.oo, 1)
+    if has_next:
+        te.wait_ge(S.qn, N_ROWS)
+        for b in range(KB):
+            te.matmul(T["p_sn%d" % b][:, 0:QP], T.ks[:, 128 * b:128 * (b + 1)], T.qn[:],
+                      start=True, stop=True).then_inc(S["sn%d" % b], 1)
+        for b in range(KB):
+            te.wait_ge(S["rn%d" % b], 1)
+            te.matmul(T.p_on[:, 0:QP], T.vs[:, 128 * b:128 * (b + 1)], T.sn_sb[:, QP * b:QP * (b + 1)],
+                      start=(b == 0), stop=(b == KB - 1)).then_inc(S.on, 1)
+
+    ve = g.vector
+    ve.memset(T.zero[:], 0.0).then_inc(S.z, 1)
+    ve.wait_ge(S.z, 1)
+    ve.wait_ge(S.so, KB)
+    ve.tensor_tensor(T.so_sb[:], T.p_so[:, 0:KB * QP], T.zero[:], AluOpType.max).then_inc(S.ro, 1)
+    if has_next:
+        for b in range(KB):
+            ve.wait_ge(S["sn%d" % b], 1)
+            ve.tensor_tensor(T.sn_sb[:, QP * b:QP * (b + 1)], T["p_sn%d" % b][:, 0:QP], T.zero[:, 0:QP],
+                             AluOpType.max).then_inc(S["rn%d" % b], 1)
+        ve.wait_ge(S.on, KB)
+        ve.tensor_copy(T.on_sb[:], T.p_on[:, 0:QP]).then_inc(S.cp, 1)
+    ve.wait_ge(S.oo, KB)
+    if has_prev:
+        ve.wait_ge(S.land, N_ROWS)
+        ve.tensor_tensor(T.ys[:], T.p_oo[:, 0:QP], T.land[:], AluOpType.add).then_inc(S.y, 1)
+    else:
+        ve.tensor_copy(T.ys[:], T.p_oo[:, 0:QP]).then_inc(S.y, 1)
+
+    g.sync.wait_ge(S.y, 1)
+    g.sync.dma_start(T.y[:], T.ys[:]).then_inc(S.st, 16)
+    g.sync.wait_ge(S.st, 16)

@@ -1,67 +1,48 @@
 from concourse.mybir import AluOpType
 
 QP, KB = 64, 4
-N_STAGE = 4
-N_ROWS = 8
+W = 128
+KV = 2 * KB * W
+PIECES = [(0, 256), (256, 512), (512, 768), (768, 1024)]
+RP = 3
 
 SCRATCH = {
-    "qd": ("dram", [128, QP], "bfloat16"),
-    "qr": ("dram", [128, QP], "bfloat16"),
     "qs": ("sbuf", [128, QP], "bfloat16"),
-    "ks": ("sbuf", [128, KB * 128], "bfloat16"),
-    "vs": ("sbuf", [128, KB * 128], "bfloat16"),
-    "qn": ("sbuf", [128, QP], "bfloat16"),
+    "kv": ("sbuf", [128, KV], "bfloat16"),
+    "kvp": ("sbuf", [128, KV], "bfloat16"),
+    "rl": ("sbuf", [128, 256], "bfloat16"),
     "zero": ("sbuf", [128, KB * QP], "float32"),
     "so_sb": ("sbuf", [128, KB * QP], "bfloat16"),
-    "sn_sb": ("sbuf", [128, KB * QP], "bfloat16"),
-    "on_sb": ("sbuf", [128, QP], "bfloat16"),
-    "land": ("sbuf", [128, QP], "bfloat16"),
+    "sp_sb": ("sbuf", [128, KB * QP], "bfloat16"),
     "ys": ("sbuf", [128, QP], "bfloat16"),
     "p_so": ("psum", [128, 512], "float32"),
-    "p_oo": ("psum", [128, 512], "float32"),
-    "p_on": ("psum", [128, 512], "float32"),
-    "p_sn0": ("psum", [128, 512], "float32"),
-    "p_sn1": ("psum", [128, 512], "float32"),
-    "p_sn2": ("psum", [128, 512], "float32"),
-    "p_sn3": ("psum", [128, 512], "float32"),
+    "p_o": ("psum", [128, 512], "float32"),
+    "p_sp0": ("psum", [128, 512], "float32"),
+    "p_sp1": ("psum", [128, 512], "float32"),
+    "p_sp2": ("psum", [128, 512], "float32"),
+    "p_sp3": ("psum", [128, 512], "float32"),
 }
-SEMAPHORES = ["qd", "q", "k", "v", "z", "so", "ro", "oo", "qn", "on", "cp", "land", "y", "st", "loc", "rel",
-              "sn0", "sn1", "sn2", "sn3", "rn0", "rn1", "rn2", "rn3"]
+SEMAPHORES = (["go", "q", "z", "so", "ro", "o", "y", "st", "loc", "rl",
+               "sp0", "sp1", "sp2", "sp3", "rp0", "rp1", "rp2", "rp3"]
+              + ["ld%d" % i for i in range(len(PIECES))] + ["ln%d" % i for i in range(len(PIECES))])
 
 
-def _routes(T, topo):
-    routes = {}
-    for r in range(1, len(T.cores)):
-        src, dst = T.cores[r], T.cores[r - 1]
-        if topo.may_write(src, dst):
-            routes[r] = [src, dst]
-        else:
-            cands = [c for c in T.cores[1:] if c != src and c != dst
-                     and topo.chip(c) == topo.chip(src) and topo.may_write(c, dst)]
-            cands.sort(key=lambda c: (topo.die(c) != topo.die(src), c))
-            routes[r] = [src, cands[0], dst]
-    return routes
+def _count(mask):
+    n = 0
+    while mask:
+        n += mask & 1
+        mask >>= 1
+    return n
 
 
-def _engines(T, topo, routes, core, n):
-    dests = []
-    for way in routes.values():
-        for a, b in zip(way[:-1], way[1:]):
-            if a == core:
-                dests.append(b)
-    r = T.rank_of(core)
-    if r + 1 < len(T.cores):
-        dests.append(T.cores[r + 1])
-    common = -1
-    for d in dests:
-        common &= topo.mask(core, d)
-    out, got, bit = 0, 0, 1
-    while got < n:
-        if common & bit:
-            out |= bit
-            got += 1
-        bit <<= 1
-    return out
+def _helper(T, topo, r):
+    src, dst = T.cores[r], T.cores[r + 1]
+    if topo.chip(src) == topo.chip(dst):
+        return None
+    cands = [c for i, c in enumerate(T.cores[:-1]) if c != src and c != dst and topo.chip(c) == topo.chip(src)
+             and topo.may_write(c, dst) and topo.chip(T.cores[i + 1]) == topo.chip(c)]
+    cands.sort(key=lambda c: (topo.die(c) == topo.die(src), c))
+    return cands[0] if cands else None
 
 
 def rank_program(g, core, T, topo):
@@ -71,77 +52,90 @@ def rank_program(g, core, T, topo):
     S = T.sem
     n = len(T.cores)
     has_prev, has_next = rank > 0, rank + 1 < n
-    routes = _routes(T, topo)
-    passes = [way for way in routes.values() if len(way) == 3 and way[1] == core]
+    half = KB * W
+    helper = _helper(T, topo, rank) if has_next else None
+    passes = [r for r in range(n - 1) if _helper(T, topo, r) == core]
+    order = [0, RP, 1, 2] if helper is not None else [0, 1, 2, 3]
 
-    def send(dst_core, out_ap, in_ap, sem, n_eng):
-        rid, pid, _ = topo.addr(dst_core)
-        g.remote_dma(out_ap, in_ap, sem, S.loc, pid, rid, _engines(T, topo, routes, core, n_eng))
-        return n_eng
-
-    if has_prev:
-        g.sync.dma_start(T.qd[0:64, :], T.q[0:64, :]).then_inc(S.qd, 16)
-        g.scalar.dma_start(T.qd[64:128, :], T.q[64:128, :]).then_inc(S.qd, 16)
+    g.scalar.wait_ge(S.go, 1)
+    for i, j in enumerate(order):
+        a, b = PIECES[j]
+        src = T.k[:, a:b] if b <= half else T.v[:, a - half:b - half]
+        (g.scalar if i % 2 else g.sync).dma_start(T.kv[:, a:b], src).then_inc(S["ld%d" % j], 16)
+        if i == 0:
+            g.sync.sem_inc(S.go, 1)
     g.sync.dma_start(T.qs[:], T.q[:]).then_inc(S.q, 16)
-    g.sync.dma_start(T.ks[:], T.k[:]).then_inc(S.k, 16)
-    g.scalar.dma_start(T.vs[:], T.v[:]).then_inc(S.v, 16)
 
     left = 0
-    if has_prev:
-        way = routes[rank]
-        g.wait_ge(S.qd, 32)
-        if len(way) == 2:
-            left += send(way[1], T.qn[:], T.qd[:], S.qn, N_ROWS)
-        else:
-            left += send(way[1], T.qr[:], T.qd[:], S.rel, N_STAGE)
-    for way in passes:
-        g.wait_ge(S.rel, N_STAGE)
-        left += send(way[2], T.qn[:], T.qr[:], S.qn, N_ROWS)
     if has_next:
-        g.wait_ge(S.cp, 1)
-        left += send(T.cores[rank + 1], T.land[:], T.on_sb[:], S.land, N_ROWS)
+        dst = T.cores[rank + 1]
+        rid, pid, _ = topo.addr(dst)
+        mask = topo.mask(core, dst)
+        for j in order:
+            a, b = PIECES[j]
+            g.wait_ge(S["ld%d" % j], 16)
+            if helper is not None and j == RP:
+                hrid, hpid, _ = topo.addr(helper)
+                hmask = topo.mask(core, helper) & ~mask
+                g.remote_dma(T.rl[:], T.kv[:, a:b], S.rl, S.loc, hpid, hrid, hmask)
+                left += _count(hmask)
+            else:
+                g.remote_dma(T.kvp[:, a:b], T.kv[:, a:b], S["ln%d" % j], S.loc, pid, rid, mask)
+                left += _count(mask)
+    for r in passes:
+        src, dst = T.cores[r], T.cores[r + 1]
+        a, b = PIECES[RP]
+        rid, pid, _ = topo.addr(dst)
+        g.wait_ge(S.rl, _count(topo.mask(src, core) & ~topo.mask(src, dst)))
+        g.remote_dma(T.kvp[:, a:b], T.rl[:], S["ln%d" % RP], S.loc, pid, rid, topo.mask(core, dst))
+        left += _count(topo.mask(core, dst))
     if left:
         g.wait_ge(S.loc, left)
 
     te = g.tensor
     te.wait_ge(S.q, 16)
-    te.wait_ge(S.k, 16)
+    te.wait_ge(S.ld0, 16)
+    te.wait_ge(S.ld1, 16)
     for b in range(KB):
-        te.matmul(T.p_so[:, QP * b:QP * (b + 1)], T.ks[:, 128 * b:128 * (b + 1)], T.qs[:],
+        te.matmul(T.p_so[:, QP * b:QP * (b + 1)], T.kv[:, W * b:W * (b + 1)], T.qs[:],
                   start=True, stop=True).then_inc(S.so, 1)
-    te.wait_ge(S.v, 16)
+    te.wait_ge(S.ld2, 16)
+    te.wait_ge(S.ld3, 16)
     te.wait_ge(S.ro, 1)
     for b in range(KB):
-        te.matmul(T.p_oo[:, 0:QP], T.vs[:, 128 * b:128 * (b + 1)], T.so_sb[:, QP * b:QP * (b + 1)],
-                  start=(b == 0), stop=(b == KB - 1)).then_inc(S.oo, 1)
-    if has_next:
-        te.wait_ge(S.qn, N_ROWS)
-        for b in range(KB):
-            te.matmul(T["p_sn%d" % b][:, 0:QP], T.ks[:, 128 * b:128 * (b + 1)], T.qn[:],
-                      start=True, stop=True).then_inc(S["sn%d" % b], 1)
-        for b in range(KB):
-            te.wait_ge(S["rn%d" % b], 1)
-            te.matmul(T.p_on[:, 0:QP], T.vs[:, 128 * b:128 * (b + 1)], T.sn_sb[:, QP * b:QP * (b + 1)],
-                      start=(b == 0), stop=(b == KB - 1)).then_inc(S.on, 1)
+        te.matmul(T.p_o[:, 0:QP], T.kv[:, W * (KB + b):W * (KB + b + 1)], T.so_sb[:, QP * b:QP * (b + 1)],
+                  start=(b == 0), stop=(b == KB - 1 and not has_prev)).then_inc(S.o, 1)
+    if has_prev:
+        prev = T.cores[rank - 1]
+        via = _helper(T, topo, rank - 1)
+        s_done, o_done = 0, 0
+        for j, (a, b) in enumerate(PIECES):
+            sender = via if (via is not None and j == RP) else prev
+            te.wait_ge(S["ln%d" % j], _count(topo.mask(sender, core)))
+            while s_done < KB and W * (s_done + 1) <= b:
+                c = s_done
+                te.matmul(T["p_sp%d" % c][:, 0:QP], T.kvp[:, W * c:W * (c + 1)], T.qs[:],
+                          start=True, stop=True).then_inc(S["sp%d" % c], 1)
+                s_done += 1
+            while o_done < KB and W * (KB + o_done + 1) <= b:
+                c = o_done
+                te.wait_ge(S["rp%d" % c], 1)
+                te.matmul(T.p_o[:, 0:QP], T.kvp[:, W * (KB + c):W * (KB + c + 1)], T.sp_sb[:, QP * c:QP * (c + 1)],
+                          start=False, stop=(c == KB - 1)).then_inc(S.o, 1)
+                o_done += 1
 
     ve = g.vector
     ve.memset(T.zero[:], 0.0).then_inc(S.z, 1)
     ve.wait_ge(S.z, 1)
     ve.wait_ge(S.so, KB)
     ve.tensor_tensor(T.so_sb[:], T.p_so[:, 0:KB * QP], T.zero[:], AluOpType.max).then_inc(S.ro, 1)
-    if has_next:
-        for b in range(KB):
-            ve.wait_ge(S["sn%d" % b], 1)
-            ve.tensor_tensor(T.sn_sb[:, QP * b:QP * (b + 1)], T["p_sn%d" % b][:, 0:QP], T.zero[:, 0:QP],
-                             AluOpType.max).then_inc(S["rn%d" % b], 1)
-        ve.wait_ge(S.on, KB)
-        ve.tensor_copy(T.on_sb[:], T.p_on[:, 0:QP]).then_inc(S.cp, 1)
-    ve.wait_ge(S.oo, KB)
     if has_prev:
-        ve.wait_ge(S.land, N_ROWS)
-        ve.tensor_tensor(T.ys[:], T.p_oo[:, 0:QP], T.land[:], AluOpType.add).then_inc(S.y, 1)
-    else:
-        ve.tensor_copy(T.ys[:], T.p_oo[:, 0:QP]).then_inc(S.y, 1)
+        for b in range(KB):
+            ve.wait_ge(S["sp%d" % b], 1)
+            ve.tensor_tensor(T.sp_sb[:, QP * b:QP * (b + 1)], T["p_sp%d" % b][:, 0:QP], T.zero[:, 0:QP],
+                             AluOpType.max).then_inc(S["rp%d" % b], 1)
+    ve.wait_ge(S.o, 2 * KB if has_prev else KB)
+    ve.tensor_copy(T.ys[:], T.p_o[:, 0:QP]).then_inc(S.y, 1)
 
     g.sync.wait_ge(S.y, 1)
     g.sync.dma_start(T.y[:], T.ys[:]).then_inc(S.st, 16)

from concourse.mybir import AluOpType

QP, KB = 64, 4
W = 128
KV = 2 * KB * W
PIECES = [(0, 256), (256, 512), (512, 768), (768, 1024)]
RP = 3

SCRATCH = {
    "qs": ("sbuf", [128, QP], "bfloat16"),
    "kv": ("sbuf", [128, KV], "bfloat16"),
    "kvp": ("sbuf", [128, KV], "bfloat16"),
    "rl": ("sbuf", [128, 256], "bfloat16"),
    "zero": ("sbuf", [128, KB * QP], "float32"),
    "so_sb": ("sbuf", [128, KB * QP], "bfloat16"),
    "sp_sb": ("sbuf", [128, KB * QP], "bfloat16"),
    "ys": ("sbuf", [128, QP], "bfloat16"),
    "p_so": ("psum", [128, 512], "float32"),
    "p_o": ("psum", [128, 512], "float32"),
    "p_sp0": ("psum", [128, 512], "float32"),
    "p_sp1": ("psum", [128, 512], "float32"),
    "p_sp2": ("psum", [128, 512], "float32"),
    "p_sp3": ("psum", [128, 512], "float32"),
}
SEMAPHORES = (["go", "q", "z", "so", "ro", "o", "y", "st", "loc", "rl",
               "sp0", "sp1", "sp2", "sp3", "rp0", "rp1", "rp2", "rp3"]
              + ["ld%d" % i for i in range(len(PIECES))] + ["ln%d" % i for i in range(len(PIECES))])


def _count(mask):
    n = 0
    while mask:
        n += mask & 1
        mask >>= 1
    return n


def _helper(T, topo, r):
    src, dst = T.cores[r], T.cores[r + 1]
    if topo.chip(src) == topo.chip(dst):
        return None
    cands = [c for i, c in enumerate(T.cores[:-1]) if c != src and c != dst and topo.chip(c) == topo.chip(src)
             and topo.may_write(c, dst) and topo.chip(T.cores[i + 1]) == topo.chip(c)]
    cands.sort(key=lambda c: (topo.die(c) == topo.die(src), c))
    return cands[0] if cands else None


def rank_program(g, core, T, topo):
    rank = T.rank_of(core)
    if rank is None:
        return
    S = T.sem
    n = len(T.cores)
    has_prev, has_next = rank > 0, rank + 1 < n
    half = KB * W
    helper = _helper(T, topo, rank) if has_next else None
    passes = [r for r in range(n - 1) if _helper(T, topo, r) == core]
    order = [0, RP, 1, 2] if helper is not None else [0, 1, 2, 3]

    g.scalar.wait_ge(S.go, 1)
    for i, j in enumerate(order):
        a, b = PIECES[j]
        src = T.k[:, a:b] if b <= half else T.v[:, a - half:b - half]
        (g.scalar if i % 2 else g.sync).dma_start(T.kv[:, a:b], src).then_inc(S["ld%d" % j], 16)
        if i == 0:
            g.sync.sem_inc(S.go, 1)
    g.sync.dma_start(T.qs[:], T.q[:]).then_inc(S.q, 16)

    left = 0
    if has_next:
        dst = T.cores[rank + 1]
        rid, pid, _ = topo.addr(dst)
        mask = topo.mask(core, dst)
        for j in order:
            a, b = PIECES[j]
            g.wait_ge(S["ld%d" % j], 16)
            if helper is not None and j == RP:
                hrid, hpid, _ = topo.addr(helper)
                hmask = topo.mask(core, helper) & ~mask
                g.remote_dma(T.rl[:], T.kv[:, a:b], S.rl, S.loc, hpid, hrid, hmask)
                left += _count(hmask)
            else:
                g.remote_dma(T.kvp[:, a:b], T.kv[:, a:b], S["ln%d" % j], S.loc, pid, rid, mask)
                left += _count(mask)
    for r in passes:
        src, dst = T.cores[r], T.cores[r + 1]
        a, b = PIECES[RP]
        rid, pid, _ = topo.addr(dst)
        g.wait_ge(S.rl, _count(topo.mask(src, core) & ~topo.mask(src, dst)))
        g.remote_dma(T.kvp[:, a:b], T.rl[:], S["ln%d" % RP], S.loc, pid, rid, topo.mask(core, dst))
        left += _count(topo.mask(core, dst))
    if left:
        g.wait_ge(S.loc, left)

    te = g.tensor
    te.wait_ge(S.q, 16)
    te.wait_ge(S.ld0, 16)
    te.wait_ge(S.ld1, 16)
    for b in range(KB):
        te.matmul(T.p_so[:, QP * b:QP * (b + 1)], T.kv[:, W * b:W * (b + 1)], T.qs[:],
                  start=True, stop=True).then_inc(S.so, 1)
    te.wait_ge(S.ld2, 16)
    te.wait_ge(S.ld3, 16)
    te.wait_ge(S.ro, 1)
    for b in range(KB):
        te.matmul(T.p_o[:, 0:QP], T.kv[:, W * (KB + b):W * (KB + b + 1)], T.so_sb[:, QP * b:QP * (b + 1)],
                  start=(b == 0), stop=(b == KB - 1 and not has_prev)).then_inc(S.o, 1)
    if has_prev:
        prev = T.cores[rank - 1]
        via = _helper(T, topo, rank - 1)
        s_done, o_done = 0, 0
        for j, (a, b) in enumerate(PIECES):
            sender = via if (via is not None and j == RP) else prev
            te.wait_ge(S["ln%d" % j], _count(topo.mask(sender, core)))
            while s_done < KB and W * (s_done + 1) <= b:
                c = s_done
                te.matmul(T["p_sp%d" % c][:, 0:QP], T.kvp[:, W * c:W * (c + 1)], T.qs[:],
                          start=True, stop=True).then_inc(S["sp%d" % c], 1)
                s_done += 1
            while o_done < KB and W * (KB + o_done + 1) <= b:
                c = o_done
                te.wait_ge(S["rp%d" % c], 1)
                te.matmul(T.p_o[:, 0:QP], T.kvp[:, W * (KB + c):W * (KB + c + 1)], T.sp_sb[:, QP * c:QP * (c + 1)],
                          start=False, stop=(c == KB - 1)).then_inc(S.o, 1)
                o_done += 1

    ve = g.vector
    ve.memset(T.zero[:], 0.0).then_inc(S.z, 1)
    ve.wait_ge(S.z, 1)
    ve.wait_ge(S.so, KB)
    ve.tensor_tensor(T.so_sb[:], T.p_so[:, 0:KB * QP], T.zero[:], AluOpType.max).then_inc(S.ro, 1)
    if has_prev:
        for b in range(KB):
            ve.wait_ge(S["sp%d" % b], 1)
            ve.tensor_tensor(T.sp_sb[:, QP * b:QP * (b + 1)], T["p_sp%d" % b][:, 0:QP], T.zero[:, 0:QP],
                             AluOpType.max).then_inc(S["rp%d" % b], 1)
    ve.wait_ge(S.o, 2 * KB if has_prev else KB)
    ve.tensor_copy(T.ys[:], T.p_o[:, 0:QP]).then_inc(S.y, 1)

    g.sync.wait_ge(S.y, 1)
    g.sync.dma_start(T.y[:], T.ys[:]).then_inc(S.st, 16)
    g.sync.wait_ge(S.st, 16)
